import numpy as np
import ml_dtypes


def mxq(x, axis, fmt="e4m3"):
    dtype, down = {"e4m3": (ml_dtypes.float8_e4m3fn, 7), "e5m2": (ml_dtypes.float8_e5m2, 14)}[fmt]
    v = np.moveaxis(np.asarray(x, np.float32).astype(ml_dtypes.bfloat16).astype(np.float64), axis, -1)
    blocks = v.reshape(v.shape[:-1] + (-1, 32))
    amax = np.abs(blocks).max(-1, keepdims=True)
    byte = np.maximum(np.where(amax > 0, np.frexp(amax)[1] - 1 + 127, 0) - down, 1)
    scale = np.exp2(byte - 127.0)
    codes = (blocks / scale).astype(np.float32).astype(dtype).astype(np.float64)
    return np.moveaxis((codes * scale).reshape(v.shape), -1, axis)


WIDE = False


def mx_kscale(k):
    if not WIDE:
        return np.ones(k)
    levels = np.array([10, -10, 5, -5, 0])
    if k % 512:
        return np.exp2(np.random.permutation(np.resize(levels, k // 32))).repeat(32)
    a = np.empty((k // 512, 16))
    for p in range(k // 512):
        a[p, :8] = np.random.permutation(np.resize(levels, 8))
        for g in range(8):
            far = levels[np.abs(levels - a[p, g]) >= 10]
            a[p, g + 8] = far[np.random.randint(len(far))]
    return np.exp2(a.ravel()).repeat(32)


def f64(x):
    return np.asarray(x).astype(np.float64)


def striped(idx):
    return np.tile(idx.reshape(-1, 16).T, (8, 1)).astype(np.uint16)


def unstriped(offs):
    return offs[:16].T.reshape(-1).astype(np.int64)


def striped8(idx):
    return np.concatenate([x.reshape(-1, 16).T for x in idx]).astype(np.uint16)


def runs(offs, k):
    lists = np.stack([offs[16 * r : 16 * r + 16].T.reshape(-1) for r in range(8)]).astype(np.int64)
    return lists[np.arange(k) % 512 // 64]


def pack_weight(w):
    k, n = w.shape
    w = f64(np.asarray(w, np.float32).astype(ml_dtypes.bfloat16)).reshape(k // 32, 32, n)
    amax = np.abs(w).max(1)
    byte = np.clip(np.where(amax > 0, np.frexp(amax)[1] - 1 + 127 - 7, 1), 1, 254)
    scaled = (w * np.exp2(127.0 - byte)[:, None, :]).reshape(k, n).astype(np.float32)
    words = np.ascontiguousarray(scaled.reshape(k // 512, 128, 4, n).transpose(0, 1, 3, 2)).astype(ml_dtypes.float8_e4m3fn).view(np.uint8)
    return words, np.ascontiguousarray(byte.astype(np.uint8).reshape(k // 512, 16, n))


def unpack_weight(words, scales):
    g, p, n, _ = words.shape
    vals = np.ascontiguousarray(words).view(ml_dtypes.float8_e4m3fn).astype(np.float64) * np.repeat(np.exp2(scales.astype(np.float64) - 127.0), 8, axis=1)[..., None]
    return vals.transpose(0, 1, 3, 2).reshape(g * 512, n)


K, T, S, N, H = 512, 2048, 512, 512, 512


def setup_inputs():
    n = np.random.standard_normal
    s = mx_kscale(K)[:, None]
    u = mx_kscale(H)
    packed_xT = pack_weight(n((K, T)) * s)
    return {
        "x_words": packed_xT[0],
        "x_scales": packed_xT[1],
        "w1": (n((K, H)) / np.sqrt(K) / s).astype(np.float32),
        "gn": (np.random.uniform(0.5, 1.5, (H, 1)) * u[:, None]).astype(np.float32),
        "w2": (n((H, H)) / np.sqrt(H) / u[:, None]).astype(np.float32),
        "res": n((N, S)).astype(np.float32),
        "w3": (n((H, N)) / np.sqrt(H) / u[:, None]).astype(np.float32),
        "offs": striped(np.random.permutation(T)[:S]),
        "d1": striped8(np.stack([np.random.permutation(S) for _ in range(8)])),
        "d2": striped8(np.stack([np.random.permutation(S) for _ in range(8)])),
        "mv": striped8(np.stack([np.random.permutation(S) for _ in range(8)])),
    }


def reference(x_words, x_scales, w1, gn, w2, res, w3, offs, d1, d2, mv):
    xq = unpack_weight(x_words, x_scales)[:, unstriped(offs)]
    y = mxq(f64(w1), 0, "e4m3").T @ xq
    v1 = y - (0.5 * (y[np.arange(H)[:, None], runs(d1, H)]))
    w = 0.5 * v1 + v1[np.arange(H)[:, None], runs(d1, H)]
    u1 = w - (0.25 * (w[np.arange(H)[:, None], runs(d2, H)]))
    z = f64(gn) * (0.25 * u1 + u1[np.arange(H)[:, None], runs(d2, H)])
    h = np.tanh(mxq(f64(w2), 0, "e4m3").T @ mxq(z, 0, "e4m3"))
    z2 = f64(gn) * (h[np.arange(H)[:, None], runs(mv, H)])
    return f64(res) + (mxq(f64(w3), 0, "e4m3").T @ mxq(z2, 0, "e4m3"))

@@ -1,0 +1,160 @@
+from contextlib import ExitStack
+
+import concourse.mybir as mybir
+
+F32 = mybir.dt.float32
+BF16 = mybir.dt.bfloat16
+I32 = mybir.dt.int32
+U32 = mybir.dt.uint32
+U16 = mybir.dt.uint16
+U8 = mybir.dt.uint8
+FP8X4 = mybir.dt.float8_e4m3fn_x4
+ALU = mybir.AluOpType
+ACT = mybir.ActivationFunctionType
+
+P = 128
+PACK = 4
+K, T, S, N, H = 512, 2048, 512, 512, 512
+FLOPS = 2 * S * (K * H + H * H + H * N)
+
+
+def tile_picked_allpass2_none_p_kernel(
+    tc, x_words, x_scales, w1, gn, w2, res, w3, offs, d1, d2, mv, out
+):
+    nc = tc.nc
+    with ExitStack() as ctx:
+        keep = ctx.enter_context(tc.tile_pool(name="keep", bufs=1))
+        psum = ctx.enter_context(tc.psum_pool(name="psum", bufs=1))
+
+        def sb(name, shape, dtype):
+            return keep.tile(shape, dtype, name=name, align_bytes=64)
+
+        offs_sb = sb("offs_sb", [P, S // 16], U16)
+        d1_sb = sb("d1_sb", [P, S // 16], U16)
+        d2_sb = sb("d2_sb", [P, S // 16], U16)
+        mv_sb = sb("mv_sb", [P, S // 16], U16)
+        xw = sb("xw", [P, T], I32)
+        xs = sb("xs", [P, T], U8)
+        xw_g = sb("xw_g", [P, S], U32)
+        xs_g = sb("xs_g", [P, S], U8)
+        gn_sb = sb("gn_sb", [P, PACK], F32)
+        gn8 = sb("gn8", [P, PACK], F32)
+        gn4 = sb("gn4", [P, PACK], F32)
+        w1_raw = [sb("w1_raw%d" % a, [P, PACK, H // 2], F32) for a in range(2)]
+        w2_raw = sb("w2_raw", [P, PACK, H], F32)
+        w3_raw = sb("w3_raw", [P, PACK, N], F32)
+        res_sb = sb("res_sb", [P, PACK, S], F32)
+        win = [[sb("win%d_%d" % (a, t), [P, 2 * S], F32) for t in range(PACK)] for a in range(2)]
+        warm = sb("warm", [P, 1], F32)
+        warm2 = sb("warm2", [P, 1], F32)
+
+        nc.vector.memset(xs[:].bitcast(I32), 0)
+        nc.vector.memset(warm[:], 0.0)
+        nc.sync.dma_start(offs_sb[:], offs)
+        nc.sync.dma_start(xw[:], x_words[0].rearrange("p n r -> p (n r)").bitcast(I32))
+        for q in range(4):
+            nc.scalar.dma_start(xs[32 * q : 32 * q + 4, :].bitcast(I32), x_scales[0, 4 * q : 4 * q + 4, :].bitcast(I32))
+        nc.scalar.activation(warm2[:], warm[:], ACT.Tanh)
+        w1_v = w1.rearrange("(p j) c -> p j c", j=PACK)
+        for a in range(2):
+            nc.sync.dma_start(w1_raw[a][:], w1_v[:, :, a * (H // 2) : (a + 1) * (H // 2)])
+        nc.sync.dma_start(gn_sb[:], gn.rearrange("(p t) o -> p (t o)", t=PACK))
+        nc.sync.dma_start(d1_sb[:], d1)
+        nc.sync.dma_start(d2_sb[:], d2)
+        nc.sync.dma_start(w2_raw[:], w2.rearrange("(p j) c -> p j c", j=PACK))
+        nc.sync.dma_start(mv_sb[:], mv)
+        nc.sync.dma_start(w3_raw[:], w3.rearrange("(p j) c -> p j c", j=PACK))
+        nc.sync.dma_start(res_sb[:], res.rearrange("(m p) j -> p m j", p=P))
+        for a in range(2):
+            for t in range(PACK):
+                nc.vector.memset(win[a][t][:, S:], 0.0)
+
+        nc.vector.tensor_copy(xs_g[:], xs[:].indirect(offs_sb[:]))
+        nc.vector.tensor_copy(xw_g[:], xw[:].bitcast(U32).indirect(offs_sb[:]))
+
+        def dealt_copy(copy, dst, raw, m0, m1, r0):
+            copy(
+                dst[:].rearrange("p (t m j) -> p m j t", t=PACK, j=PACK)[:, m0:m1],
+                raw[:].rearrange("p j (m t) -> p m j t", t=PACK)[:, m0 - r0 : m1 - r0],
+            )
+
+        w1_b = sb("w1_b", [P, PACK * H], BF16)
+        w1_c = sb("w1_c", [P, H], U32)
+        w1_s = sb("w1_s", [P, H], U8)
+        dealt_copy(nc.scalar.copy, w1_b, w1_raw[0], 0, 64, 0)
+        dealt_copy(nc.vector.tensor_copy, w1_b, w1_raw[1], 64, 128, 64)
+        nc.vector.tensor_scalar(gn8[:], gn_sb[:], 0.125, None, ALU.mult)
+        nc.vector.tensor_scalar(gn4[:], gn_sb[:], 0.25, None, ALU.mult)
+
+        banks = [psum.tile([P, S], F32, name="bank%d" % b) for b in range(8)]
+        side = [sb("side%d" % t, [P, S], F32) for t in range(PACK)]
+        for t in range(PACK):
+            cols = slice(t * P, (t + 1) * P)
+            nc.vector.quantize_mx(w1_c[:, cols].bitcast(FP8X4), w1_s[:, cols], w1_b[:, t * 512 : (t + 1) * 512])
+            nc.tensor.matmul_mx(banks[t][:], lhsT=w1_c[:, cols].bitcast(FP8X4), lhsT_scale=w1_s[:, cols],
+                                rhs=xw_g[:].bitcast(FP8X4), rhs_scale=xs_g[:], start=True, stop=True)
+            nc.scalar.activation(win[0][t][:, :S], banks[t][:], ACT.Copy, scale=gn8[:, t : t + 1])
+            nc.scalar.activation(side[t][:], banks[t][:], ACT.Copy, scale=gn4[:, t : t + 1])
+
+        w2_b = sb("w2_b", [P, PACK * H], BF16)
+        w2_c = sb("w2_c", [P, H], U32)
+        w2_s = sb("w2_s", [P, H], U8)
+        w3_b = sb("w3_b", [P, PACK * N], BF16)
+        w3_c = sb("w3_c", [P, N], U32)
+        w3_s = sb("w3_s", [P, N], U8)
+        last_side = sb("last_side", [P, PACK, S], F32)
+        last_g = sb("last_g", [P, PACK, S], F32)
+
+        def weave(t4):
+            return t4.rearrange("p t (c i) -> p c t i", i=4)
+
+        def woven(flat):
+            return flat.rearrange("p (c i t) -> p c t i", i=4, t=PACK)
+
+        for t in range(PACK):
+            nc.vector.tensor_tensor(win[1][t][:, :S], win[0][t][:].indirect(d1_sb[:]), side[t][:], ALU.subtract)
+            nc.scalar.mul(side[t][:], win[1][t][:, :S], 0.5)
+            dealt_copy(nc.scalar.copy, w2_b, w2_raw, 32 * t, 32 * t + 32, 0)
+        for t in range(PACK):
+            nc.vector.tensor_tensor(win[0][t][:, :S], win[1][t][:].indirect(d1_sb[:]), side[t][:], ALU.add)
+            nc.scalar.mul(side[t][:], win[0][t][:, :S], 4.0)
+            nc.scalar.copy(woven(w3_b[:, t * 512 : (t + 1) * 512]), weave(w3_raw[:, :, t * P : (t + 1) * P]))
+        nc.vector.quantize_mx(w2_c[:].bitcast(FP8X4), w2_s[:], w2_b[:])
+        for t in range(PACK):
+            nc.vector.tensor_tensor(win[1][t][:, :S], win[0][t][:].indirect(d2_sb[:]), side[t][:], ALU.subtract)
+            nc.scalar.mul(last_side[:, t, :], win[1][t][:, :S], 0.25)
+        nc.vector.quantize_mx(w3_c[:].bitcast(FP8X4), w3_s[:], w3_b[:])
+        for t in range(PACK):
+            nc.vector.tensor_copy(last_g[:, t, :], win[1][t][:].indirect(d2_sb[:]))
+
+        z_b = sb("z_b", [P, PACK * S], BF16)
+        z_c = sb("z_c", [P, S], U32)
+        z_s = sb("z_s", [P, S], U8)
+        nc.vector.tensor_tensor(woven(z_b[:]), weave(last_g[:]), weave(last_side[:]), ALU.add)
+        nc.vector.quantize_mx(z_c[:].bitcast(FP8X4), z_s[:], z_b[:])
+
+        h_g = sb("h_g", [P, PACK, S], F32)
+        for t in range(PACK):
+            cols = slice(t * P, (t + 1) * P)
+            nc.tensor.matmul_mx(banks[4 + t][:], lhsT=w2_c[:, cols].bitcast(FP8X4), lhsT_scale=w2_s[:, cols],
+                                rhs=z_c[:].bitcast(FP8X4), rhs_scale=z_s[:], start=True, stop=True)
+            nc.scalar.activation(side[t][:], banks[4 + t][:], ACT.Tanh)
+            if t == 0:
+                nc.vector.tensor_scalar(win[0][t][:, :S], side[t][:], gn_sb[:, t : t + 1], None, ALU.mult)
+            else:
+                nc.scalar.activation(win[0][t][:, :S], side[t][:], ACT.Copy, scale=gn_sb[:, t : t + 1])
+            nc.vector.tensor_copy(h_g[:, t, :], win[0][t][:].indirect(mv_sb[:]))
+
+        z2_b = sb("z2_b", [P, PACK * S], BF16)
+        z2_c = sb("z2_c", [P, S], U32)
+        z2_s = sb("z2_s", [P, S], U8)
+        nc.vector.tensor_copy(woven(z2_b[:]), weave(h_g[:]))
+        nc.vector.quantize_mx(z2_c[:].bitcast(FP8X4), z2_s[:], z2_b[:])
+
+        for m in range(PACK):
+            cols = slice(m * P, (m + 1) * P)
+            nc.tensor.matmul_mx(banks[m][:], lhsT=w3_c[:, cols].bitcast(FP8X4), lhsT_scale=w3_s[:, cols],
+                                rhs=z2_c[:].bitcast(FP8X4), rhs_scale=z2_s[:], start=True, stop=True)
+            o_sb = sb("o_sb%d" % m, [P, S], F32)
+            nc.vector.tensor_tensor(o_sb[:], banks[m][:], res_sb[:, m, :], ALU.add)
+            nc.sync.dma_start(out[cols, :], o_sb[:])

@@ -40,24 +40,26 @@ def tile_picked_allpass2_none_p_kernel(
         gn_sb = sb("gn_sb", [P, PACK], F32)
         gn8 = sb("gn8", [P, PACK], F32)
         gn4 = sb("gn4", [P, PACK], F32)
-        w1_raw = [sb("w1_raw%d" % a, [P, PACK, H // 2], F32) for a in range(2)]
+        w1_raw = sb("w1_raw", [P, PACK, H], F32)
         w2_raw = sb("w2_raw", [P, PACK, H], F32)
         w3_raw = sb("w3_raw", [P, PACK, N], F32)
         res_sb = sb("res_sb", [P, PACK, S], F32)
         win = [[sb("win%d_%d" % (a, t), [P, 2 * S], F32) for t in range(PACK)] for a in range(2)]
+        HALF = S // 2
+
+        def shared(tag, name, shape, dtype):
+            return keep.tile(shape, dtype, name=name, tag=tag, align_bytes=64)
         warm = sb("warm", [P, 1], F32)
         warm2 = sb("warm2", [P, 1], F32)
 
         nc.vector.memset(xs[:].bitcast(I32), 0)
         nc.vector.memset(warm[:], 0.0)
+        nc.sync.dma_start(w1_raw[:], w1.rearrange("(p j) c -> p j c", j=PACK))
         nc.sync.dma_start(offs_sb[:], offs)
         nc.sync.dma_start(xw[:], x_words[0].rearrange("p n r -> p (n r)").bitcast(I32))
         for q in range(4):
             nc.scalar.dma_start(xs[32 * q : 32 * q + 4, :].bitcast(I32), x_scales[0, 4 * q : 4 * q + 4, :].bitcast(I32))
         nc.scalar.activation(warm2[:], warm[:], ACT.Tanh)
-        w1_v = w1.rearrange("(p j) c -> p j c", j=PACK)
-        for a in range(2):
-            nc.sync.dma_start(w1_raw[a][:], w1_v[:, :, a * (H // 2) : (a + 1) * (H // 2)])
         nc.sync.dma_start(gn_sb[:], gn.rearrange("(p t) o -> p (t o)", t=PACK))
         nc.sync.dma_start(d1_sb[:], d1)
         nc.sync.dma_start(d2_sb[:], d2)
@@ -65,12 +67,10 @@ def tile_picked_allpass2_none_p_kernel(
         nc.sync.dma_start(mv_sb[:], mv)
         nc.sync.dma_start(w3_raw[:], w3.rearrange("(p j) c -> p j c", j=PACK))
         nc.sync.dma_start(res_sb[:], res.rearrange("(m p) j -> p m j", p=P))
-        for a in range(2):
-            for t in range(PACK):
-                nc.vector.memset(win[a][t][:, S:], 0.0)
+        for t in range(PACK):
+            nc.vector.memset(win[0][t][:, S:], 0.0)
 
         nc.vector.tensor_copy(xs_g[:], xs[:].indirect(offs_sb[:]))
-        nc.vector.tensor_copy(xw_g[:], xw[:].bitcast(U32).indirect(offs_sb[:]))
 
         def dealt_copy(copy, dst, raw, m0, m1, r0):
             copy(
@@ -81,29 +81,42 @@ def tile_picked_allpass2_none_p_kernel(
         w1_b = sb("w1_b", [P, PACK * H], BF16)
         w1_c = sb("w1_c", [P, H], U32)
         w1_s = sb("w1_s", [P, H], U8)
-        dealt_copy(nc.scalar.copy, w1_b, w1_raw[0], 0, 64, 0)
-        dealt_copy(nc.vector.tensor_copy, w1_b, w1_raw[1], 64, 128, 64)
+        dealt_copy(nc.scalar.copy, w1_b, w1_raw, 0, 64, 0)
+        dealt_copy(nc.vector.tensor_copy, w1_b, w1_raw, 64, 128, 0)
         nc.vector.tensor_scalar(gn8[:], gn_sb[:], 0.125, None, ALU.mult)
         nc.vector.tensor_scalar(gn4[:], gn_sb[:], 0.25, None, ALU.mult)
 
         banks = [psum.tile([P, S], F32, name="bank%d" % b) for b in range(8)]
-        side = [sb("side%d" % t, [P, S], F32) for t in range(PACK)]
         for t in range(PACK):
             cols = slice(t * P, (t + 1) * P)
             nc.vector.quantize_mx(w1_c[:, cols].bitcast(FP8X4), w1_s[:, cols], w1_b[:, t * 512 : (t + 1) * 512])
-            nc.tensor.matmul_mx(banks[t][:], lhsT=w1_c[:, cols].bitcast(FP8X4), lhsT_scale=w1_s[:, cols],
-                                rhs=xw_g[:].bitcast(FP8X4), rhs_scale=xs_g[:], start=True, stop=True)
-            nc.scalar.activation(win[0][t][:, :S], banks[t][:], ACT.Copy, scale=gn8[:, t : t + 1])
-            nc.scalar.activation(side[t][:], banks[t][:], ACT.Copy, scale=gn4[:, t : t + 1])
+            if t == 0:
+                for h in range(2):
+                    hc = slice(h * HALF, (h + 1) * HALF)
+                    nc.vector.tensor_copy(xw_g[:, hc], xw[:].bitcast(U32).indirect(offs_sb[:, h * (HALF // 16) : (h + 1) * (HALF // 16)]))
+                    nc.tensor.matmul_mx(banks[h][:, :HALF], lhsT=w1_c[:, cols].bitcast(FP8X4), lhsT_scale=w1_s[:, cols],
+                                        rhs=xw_g[:, hc].bitcast(FP8X4), rhs_scale=xs_g[:, hc], start=True, stop=True)
+                nc.scalar.activation(win[0][0][:, :HALF], banks[0][:, :HALF], ACT.Copy, scale=gn8[:, 0:1])
+                nc.scalar.activation(win[1][0][:, S : S + HALF], banks[0][:, :HALF], ACT.Copy, scale=gn4[:, 0:1])
+                nc.vector.tensor_scalar(win[0][0][:, HALF:S], banks[1][:, :HALF], gn8[:, 0:1], None, ALU.mult)
+                nc.vector.tensor_scalar(win[1][0][:, S + HALF :], banks[1][:, :HALF], gn4[:, 0:1], None, ALU.mult)
+            else:
+                nc.tensor.matmul_mx(banks[t + 1][:], lhsT=w1_c[:, cols].bitcast(FP8X4), lhsT_scale=w1_s[:, cols],
+                                    rhs=xw_g[:].bitcast(FP8X4), rhs_scale=xs_g[:], start=True, stop=True)
+                nc.scalar.activation(win[0][t][:, :S], banks[t + 1][:], ACT.Copy, scale=gn8[:, t : t + 1])
+                nc.scalar.activation(win[1][t][:, S:], banks[t + 1][:], ACT.Copy, scale=gn4[:, t : t + 1])
+
+        gains = [shared("gains%d" % h, "gains%d" % h, [P, PACK, HALF], F32) for h in range(2)]
+        for h in range(2):
+            nc.vector.tensor_copy(gains[h][:], gn_sb[:].unsqueeze(2).to_broadcast([P, PACK, HALF]))
 
         w2_b = sb("w2_b", [P, PACK * H], BF16)
-        w2_c = sb("w2_c", [P, H], U32)
+        w2_c0 = sb("w2_c0", [P, P], U32)
         w2_s = sb("w2_s", [P, H], U8)
         w3_b = sb("w3_b", [P, PACK * N], BF16)
-        w3_c = sb("w3_c", [P, N], U32)
         w3_s = sb("w3_s", [P, N], U8)
-        last_side = sb("last_side", [P, PACK, S], F32)
-        last_g = sb("last_g", [P, PACK, S], F32)
+        u = [sb("u%d" % t, [P, S], F32) for t in range(PACK)]
+        u_side = [shared("u_side%d" % h, "u_side%d" % h, [P, PACK, HALF], F32) for h in range(2)]
 
         def weave(t4):
             return t4.rearrange("p t (c i) -> p c t i", i=4)
@@ -111,50 +124,78 @@ def tile_picked_allpass2_none_p_kernel(
         def woven(flat):
             return flat.rearrange("p (c i t) -> p c t i", i=4, t=PACK)
 
+        def half_list(lst, h):
+            return lst[:, h * (HALF // 16) : (h + 1) * (HALF // 16)]
+
         for t in range(PACK):
-            nc.vector.tensor_tensor(win[1][t][:, :S], win[0][t][:].indirect(d1_sb[:]), side[t][:], ALU.subtract)
-            nc.scalar.mul(side[t][:], win[1][t][:, :S], 0.5)
+            nc.vector.tensor_tensor(win[1][t][:, :S], win[0][t][:].indirect(d1_sb[:]), win[1][t][:, S:], ALU.subtract)
+            nc.scalar.mul(win[0][t][:, S:], win[1][t][:, :S], 0.5)
+        for t in range(PACK):
+            nc.vector.tensor_tensor(win[0][t][:, :S], win[1][t][:].indirect(d1_sb[:]), win[0][t][:, S:], ALU.add)
+            nc.scalar.mul(win[1][t][:, S:], win[0][t][:, :S], 4.0)
             dealt_copy(nc.scalar.copy, w2_b, w2_raw, 32 * t, 32 * t + 32, 0)
         for t in range(PACK):
-            nc.vector.tensor_tensor(win[0][t][:, :S], win[1][t][:].indirect(d1_sb[:]), side[t][:], ALU.add)
-            nc.scalar.mul(side[t][:], win[0][t][:, :S], 4.0)
+            nc.vector.tensor_tensor(u[t][:], win[0][t][:].indirect(d2_sb[:]), win[1][t][:, S:], ALU.subtract)
+            for h in range(2):
+                nc.scalar.mul(u_side[h][:, t, :], u[t][:, h * HALF : (h + 1) * HALF], 0.25)
             nc.scalar.copy(woven(w3_b[:, t * 512 : (t + 1) * 512]), weave(w3_raw[:, :, t * P : (t + 1) * P]))
-        nc.vector.quantize_mx(w2_c[:].bitcast(FP8X4), w2_s[:], w2_b[:])
-        for t in range(PACK):
-            nc.vector.tensor_tensor(win[1][t][:, :S], win[0][t][:].indirect(d2_sb[:]), side[t][:], ALU.subtract)
-            nc.scalar.mul(last_side[:, t, :], win[1][t][:, :S], 0.25)
-        nc.vector.quantize_mx(w3_c[:].bitcast(FP8X4), w3_s[:], w3_b[:])
-        for t in range(PACK):
-            nc.vector.tensor_copy(last_g[:, t, :], win[1][t][:].indirect(d2_sb[:]))
+        nc.vector.quantize_mx(w2_c0[:].bitcast(FP8X4), w2_s[:, :P], w2_b[:, :512])
 
-        z_b = sb("z_b", [P, PACK * S], BF16)
         z_c = sb("z_c", [P, S], U32)
         z_s = sb("z_s", [P, S], U8)
-        nc.vector.tensor_tensor(woven(z_b[:]), weave(last_g[:]), weave(last_side[:]), ALU.add)
-        nc.vector.quantize_mx(z_c[:].bitcast(FP8X4), z_s[:], z_b[:])
+        for h in range(2):
+            hc = slice(h * HALF, (h + 1) * HALF)
+            z_f = sb("z_f", [P, PACK, HALF], F32) if h == 0 else shared("u_side0", "z_f1", [P, PACK, HALF], F32)
+            for t in range(PACK):
+                nc.vector.tensor_tensor(z_f[:, t, :], u[t][:].indirect(half_list(d2_sb, h)), u_side[h][:, t, :], ALU.add)
+            z_b = shared("z_b", "z_b%d" % h, [P, PACK * HALF], BF16)
+            (nc.scalar.copy if h == 0 else nc.vector.tensor_copy)(woven(z_b[:]), weave(z_f[:]))
+            nc.vector.quantize_mx(z_c[:, hc].bitcast(FP8X4), z_s[:, hc], z_b[:])
 
-        h_g = sb("h_g", [P, PACK, S], F32)
+        late_c = shared("z_b", "late_c", [P, 3 * P + N], U32)
+        a_banks = [banks[5], banks[6], banks[7], banks[0]]
+        hwin = [sb("hwin%d" % t, [P, S], F32) for t in range(PACK)]
         for t in range(PACK):
             cols = slice(t * P, (t + 1) * P)
-            nc.tensor.matmul_mx(banks[4 + t][:], lhsT=w2_c[:, cols].bitcast(FP8X4), lhsT_scale=w2_s[:, cols],
-                                rhs=z_c[:].bitcast(FP8X4), rhs_scale=z_s[:], start=True, stop=True)
-            nc.scalar.activation(side[t][:], banks[4 + t][:], ACT.Tanh)
             if t == 0:
-                nc.vector.tensor_scalar(win[0][t][:, :S], side[t][:], gn_sb[:, t : t + 1], None, ALU.mult)
+                codes = w2_c0[:]
             else:
-                nc.scalar.activation(win[0][t][:, :S], side[t][:], ACT.Copy, scale=gn_sb[:, t : t + 1])
-            nc.vector.tensor_copy(h_g[:, t, :], win[0][t][:].indirect(mv_sb[:]))
+                codes = late_c[:, (t - 1) * P : t * P]
+                nc.vector.quantize_mx(codes.bitcast(FP8X4), w2_s[:, cols], w2_b[:, t * 512 : (t + 1) * 512])
+            for h in range(2):
+                hc = slice(h * HALF, (h + 1) * HALF)
+                bank = banks[1] if (t, h) == (0, 0) else a_banks[t]
+                nc.tensor.matmul_mx(bank[:, hc], lhsT=codes.bitcast(FP8X4), lhsT_scale=w2_s[:, cols],
+                                    rhs=z_c[:, hc].bitcast(FP8X4), rhs_scale=z_s[:, hc], start=True, stop=True)
+                if t == 0:
+                    nc.scalar.activation(hwin[t][:, hc], bank[:, hc], ACT.Tanh)
+            if t > 0:
+                nc.scalar.activation(hwin[t][:], a_banks[t][:], ACT.Tanh)
+        w3_c = late_c[:, 3 * P :]
+        nc.vector.quantize_mx(w3_c.bitcast(FP8X4), w3_s[:], w3_b[:])
 
-        z2_b = sb("z2_b", [P, PACK * S], BF16)
         z2_c = sb("z2_c", [P, S], U32)
         z2_s = sb("z2_s", [P, S], U8)
-        nc.vector.tensor_copy(woven(z2_b[:]), weave(h_g[:]))
-        nc.vector.quantize_mx(z2_c[:].bitcast(FP8X4), z2_s[:], z2_b[:])
-
-        for m in range(PACK):
-            cols = slice(m * P, (m + 1) * P)
-            nc.tensor.matmul_mx(banks[m][:], lhsT=w3_c[:, cols].bitcast(FP8X4), lhsT_scale=w3_s[:, cols],
-                                rhs=z2_c[:].bitcast(FP8X4), rhs_scale=z2_s[:], start=True, stop=True)
-            o_sb = sb("o_sb%d" % m, [P, S], F32)
-            nc.vector.tensor_tensor(o_sb[:], banks[m][:], res_sb[:, m, :], ALU.add)
-            nc.sync.dma_start(out[cols, :], o_sb[:])
+        out_v = out.rearrange("(m p) j -> p m j", p=P)
+        for h in range(2):
+            hc = slice(h * HALF, (h + 1) * HALF)
+            z2_f = sb("z2_f", [P, PACK, HALF], F32) if h == 0 else shared("gains0", "z2_f1", [P, PACK, HALF], F32)
+            for t in range(PACK):
+                nc.vector.tensor_tensor(z2_f[:, t, :], hwin[t][:].indirect(half_list(mv_sb, h)), gains[h][:, t, :], ALU.mult)
+            z2_b = shared("z2_b", "z2_b%d" % h, [P, PACK * HALF], BF16)
+            (nc.scalar.copy if h == 0 else nc.vector.tensor_copy)(woven(z2_b[:]), weave(z2_f[:]))
+            nc.vector.quantize_mx(z2_c[:, hc].bitcast(FP8X4), z2_s[:, hc], z2_b[:])
+        for h in range(2):
+            hc = slice(h * HALF, (h + 1) * HALF)
+            for a in range(2):
+                bank = banks[1 + 2 * h + a]
+                for e in range(2):
+                    m = 2 * a + e
+                    cols = slice(m * P, (m + 1) * P)
+                    nc.tensor.matmul_mx(bank[:, e * HALF : (e + 1) * HALF], lhsT=w3_c[:, cols].bitcast(FP8X4), lhsT_scale=w3_s[:, cols],
+                                        rhs=z2_c[:, hc].bitcast(FP8X4), rhs_scale=z2_s[:, hc], start=True, stop=True)
+                for e0, e1 in ((0, 1), (1, 2)) if (h, a) == (1, 1) else ((0, 2),):
+                    o_sb = sb("o_sb%d_%d_%d" % (h, a, e0), [P, e1 - e0, HALF], F32)
+                    rows = slice(2 * a + e0, 2 * a + e1)
+                    nc.vector.tensor_tensor(o_sb[:], bank[:].rearrange("p (e j) -> p e j", e=2)[:, e0:e1], res_sb[:, rows, hc], ALU.add)
+                    nc.sync.dma_start(out_v[:, rows, hc], o_sb[:])

@@ -35,42 +35,37 @@ def tile_picked_allpass2_none_p_kernel(
         mv_sb = sb("mv_sb", [P, S // 16], U16)
         xw = sb("xw", [P, T], I32)
         xs = sb("xs", [P, T], U8)
-        xw_g = sb("xw_g", [P, S], U32)
-        xs_g = sb("xs_g", [P, S], U8)
+        xw_g = keep.tile([P, S], U32, name="xw_g", tag="xw_g", align_bytes=64)
+        xs_g = keep.tile([P, S], U8, name="xs_g", tag="gains0", align_bytes=64)
         gn_sb = sb("gn_sb", [P, PACK], F32)
         gn8 = sb("gn8", [P, PACK], F32)
         gn4 = sb("gn4", [P, PACK], F32)
-        w1_raw = sb("w1_raw", [P, PACK, H], F32)
-        w2_raw = sb("w2_raw", [P, PACK, H], F32)
-        w3_raw = sb("w3_raw", [P, PACK, N], F32)
-        res_sb = sb("res_sb", [P, PACK, S], F32)
+        w1_raw = [keep.tile([P, PACK, H // 2], F32, name="w1_raw%d" % a, tag="w_raw%d" % a, align_bytes=64) for a in range(2)]
         win = [[sb("win%d_%d" % (a, t), [P, 2 * S], F32) for t in range(PACK)] for a in range(2)]
         HALF = S // 2
 
         def shared(tag, name, shape, dtype):
             return keep.tile(shape, dtype, name=name, tag=tag, align_bytes=64)
-        warm = sb("warm", [P, 1], F32)
-        warm2 = sb("warm2", [P, 1], F32)
 
         nc.vector.memset(xs[:].bitcast(I32), 0)
-        nc.vector.memset(warm[:], 0.0)
-        nc.sync.dma_start(w1_raw[:], w1.rearrange("(p j) c -> p j c", j=PACK))
-        nc.sync.dma_start(offs_sb[:], offs)
-        nc.sync.dma_start(xw[:], x_words[0].rearrange("p n r -> p (n r)").bitcast(I32))
+        xs_rows = sb("xs_rows", [P, T // 4], I32)
         for q in range(4):
-            nc.scalar.dma_start(xs[32 * q : 32 * q + 4, :].bitcast(I32), x_scales[0, 4 * q : 4 * q + 4, :].bitcast(I32))
-        nc.scalar.activation(warm2[:], warm[:], ACT.Tanh)
+            (nc.sync, nc.scalar)[q % 2].dma_start(xs_rows[32 * q : 32 * q + 4, :], x_scales[0, 4 * q : 4 * q + 4, :].bitcast(I32))
+        nc.sync.dma_start(xw[:], x_words[0].rearrange("p n r -> p (n r)").bitcast(I32))
+        nc.sync.dma_start(offs_sb[:], offs)
+        for a in range(2):
+            nc.sync.dma_start(w1_raw[a][:], w1.rearrange("(p j) c -> p j c", j=PACK)[:, :, a * (H // 2) : (a + 1) * (H // 2)])
         nc.sync.dma_start(gn_sb[:], gn.rearrange("(p t) o -> p (t o)", t=PACK))
         nc.sync.dma_start(d1_sb[:], d1)
         nc.sync.dma_start(d2_sb[:], d2)
-        nc.sync.dma_start(w2_raw[:], w2.rearrange("(p j) c -> p j c", j=PACK))
         nc.sync.dma_start(mv_sb[:], mv)
-        nc.sync.dma_start(w3_raw[:], w3.rearrange("(p j) c -> p j c", j=PACK))
-        nc.sync.dma_start(res_sb[:], res.rearrange("(m p) j -> p m j", p=P))
         for t in range(PACK):
             nc.vector.memset(win[0][t][:, S:], 0.0)
 
+        for q in range(4):
+            nc.vector.tensor_copy(xs[32 * q : 32 * q + 4, :].bitcast(I32), xs_rows[32 * q : 32 * q + 4, :])
         nc.vector.tensor_copy(xs_g[:], xs[:].indirect(offs_sb[:]))
+        nc.vector.tensor_copy(xw_g[:], xw[:].bitcast(U32).indirect(offs_sb[:]))
 
         def dealt_copy(copy, dst, raw, m0, m1, r0):
             copy(
@@ -78,37 +73,38 @@ def tile_picked_allpass2_none_p_kernel(
                 raw[:].rearrange("p j (m t) -> p m j t", t=PACK)[:, m0 - r0 : m1 - r0],
             )
 
-        w1_b = sb("w1_b", [P, PACK * H], BF16)
+        w1_b = shared("w1_b", "w1_b", [P, PACK * H], BF16)
         w1_c = sb("w1_c", [P, H], U32)
-        w1_s = sb("w1_s", [P, H], U8)
-        dealt_copy(nc.scalar.copy, w1_b, w1_raw, 0, 64, 0)
-        dealt_copy(nc.vector.tensor_copy, w1_b, w1_raw, 64, 128, 0)
+        w1_s = shared("gains1", "w1_s", [P, H], U8)
+        dealt_copy(nc.scalar.copy, w1_b, w1_raw[0], 0, 64, 0)
+        dealt_copy(nc.vector.tensor_copy, w1_b, w1_raw[1], 64, 108, 64)
+        dealt_copy(nc.scalar.copy, w1_b, w1_raw[1], 108, 128, 64)
         nc.vector.tensor_scalar(gn8[:], gn_sb[:], 0.125, None, ALU.mult)
         nc.vector.tensor_scalar(gn4[:], gn_sb[:], 0.25, None, ALU.mult)
 
         banks = [psum.tile([P, S], F32, name="bank%d" % b) for b in range(8)]
         for t in range(PACK):
             cols = slice(t * P, (t + 1) * P)
-            nc.vector.quantize_mx(w1_c[:, cols].bitcast(FP8X4), w1_s[:, cols], w1_b[:, t * 512 : (t + 1) * 512])
-            if t == 0:
-                for h in range(2):
-                    hc = slice(h * HALF, (h + 1) * HALF)
-                    nc.vector.tensor_copy(xw_g[:, hc], xw[:].bitcast(U32).indirect(offs_sb[:, h * (HALF // 16) : (h + 1) * (HALF // 16)]))
-                    nc.tensor.matmul_mx(banks[h][:, :HALF], lhsT=w1_c[:, cols].bitcast(FP8X4), lhsT_scale=w1_s[:, cols],
-                                        rhs=xw_g[:, hc].bitcast(FP8X4), rhs_scale=xs_g[:, hc], start=True, stop=True)
-                nc.scalar.activation(win[0][0][:, :HALF], banks[0][:, :HALF], ACT.Copy, scale=gn8[:, 0:1])
-                nc.scalar.activation(win[1][0][:, S : S + HALF], banks[0][:, :HALF], ACT.Copy, scale=gn4[:, 0:1])
-                nc.vector.tensor_scalar(win[0][0][:, HALF:S], banks[1][:, :HALF], gn8[:, 0:1], None, ALU.mult)
-                nc.vector.tensor_scalar(win[1][0][:, S + HALF :], banks[1][:, :HALF], gn4[:, 0:1], None, ALU.mult)
-            else:
-                nc.tensor.matmul_mx(banks[t + 1][:], lhsT=w1_c[:, cols].bitcast(FP8X4), lhsT_scale=w1_s[:, cols],
-                                    rhs=xw_g[:].bitcast(FP8X4), rhs_scale=xs_g[:], start=True, stop=True)
-                nc.scalar.activation(win[0][t][:, :S], banks[t + 1][:], ACT.Copy, scale=gn8[:, t : t + 1])
-                nc.scalar.activation(win[1][t][:, S:], banks[t + 1][:], ACT.Copy, scale=gn4[:, t : t + 1])
+            if t < 3:
+                wide = slice(t * P, (t + 1) * P if t < 2 else H)
+                nc.vector.quantize_mx(w1_c[:, wide].bitcast(FP8X4), w1_s[:, wide], w1_b[:, PACK * wide.start : PACK * wide.stop])
+            pieces = ((0, HALF), (HALF, S)) if t == 0 else ((0, S),)
+            for b, (c0, c1) in enumerate(pieces):
+                bank = banks[b] if t == 0 else banks[t + 2]
+                nc.tensor.matmul_mx(bank[:, : c1 - c0], lhsT=w1_c[:, cols].bitcast(FP8X4), lhsT_scale=w1_s[:, cols],
+                                    rhs=xw_g[:, c0:c1].bitcast(FP8X4), rhs_scale=xs_g[:, c0:c1], start=True, stop=True)
+                for dst, gain in ((win[0][t][:, c0:c1], gn8), (win[1][t][:, S + c0 : S + c1], gn4)):
+                    if (t, b) == (0, 0):
+                        nc.vector.tensor_scalar(dst, bank[:, : c1 - c0], gain[:, t : t + 1], None, ALU.mult)
+                    else:
+                        nc.scalar.activation(dst, bank[:, : c1 - c0], ACT.Copy, scale=gain[:, t : t + 1])
 
-        gains = [shared("gains%d" % h, "gains%d" % h, [P, PACK, HALF], F32) for h in range(2)]
-        for h in range(2):
-            nc.vector.tensor_copy(gains[h][:], gn_sb[:].unsqueeze(2).to_broadcast([P, PACK, HALF]))
+        w2_raw = shared("w_raw1", "w2_raw", [P, PACK, H], F32)
+        w3_raw = shared("w1_b", "w3_raw", [P, PACK, N], F32)
+        res_sb = shared("xw_g", "res_sb", [P, PACK, S], F32)
+        nc.sync.dma_start(w2_raw[:], w2.rearrange("(p j) c -> p j c", j=PACK))
+        nc.sync.dma_start(w3_raw[:], w3.rearrange("(p j) c -> p j c", j=PACK))
+        nc.sync.dma_start(res_sb[:], res.rearrange("(m p) j -> p m j", p=P))
 
         w2_b = sb("w2_b", [P, PACK * H], BF16)
         w2_c0 = sb("w2_c0", [P, P], U32)
@@ -141,32 +137,36 @@ def tile_picked_allpass2_none_p_kernel(
             nc.scalar.copy(woven(w3_b[:, t * 512 : (t + 1) * 512]), weave(w3_raw[:, :, t * P : (t + 1) * P]))
         nc.vector.quantize_mx(w2_c0[:].bitcast(FP8X4), w2_s[:, :P], w2_b[:, :512])
 
-        z_c = sb("z_c", [P, S], U32)
+        gains = [shared("gains%d" % h, "gains%d" % h, [P, PACK, HALF], F32) for h in range(2)]
+        for h in range(2):
+            for a in range(2):
+                nc.scalar.copy(gains[h][:, 2 * a : 2 * a + 2], gn_sb[:, 2 * a : 2 * a + 2].unsqueeze(2).to_broadcast([P, 2, HALF]))
+
+        z_c = []
         z_s = sb("z_s", [P, S], U8)
         for h in range(2):
             hc = slice(h * HALF, (h + 1) * HALF)
             z_f = sb("z_f", [P, PACK, HALF], F32) if h == 0 else shared("u_side0", "z_f1", [P, PACK, HALF], F32)
             for t in range(PACK):
                 nc.vector.tensor_tensor(z_f[:, t, :], u[t][:].indirect(half_list(d2_sb, h)), u_side[h][:, t, :], ALU.add)
-            z_b = shared("z_b", "z_b%d" % h, [P, PACK * HALF], BF16)
+            z_b = shared("z_b%d" % h, "z_b%d" % h, [P, PACK * HALF], BF16)
             (nc.scalar.copy if h == 0 else nc.vector.tensor_copy)(woven(z_b[:]), weave(z_f[:]))
-            nc.vector.quantize_mx(z_c[:, hc].bitcast(FP8X4), z_s[:, hc], z_b[:])
+            z_c.append(sb("z_c0", [P, HALF], U32) if h == 0 else shared("z_b0", "z_c1", [P, HALF], U32))
+            nc.vector.quantize_mx(z_c[h][:].bitcast(FP8X4), z_s[:, hc], z_b[:])
 
-        late_c = shared("z_b", "late_c", [P, 3 * P + N], U32)
-        a_banks = [banks[5], banks[6], banks[7], banks[0]]
+        late_c = shared("z_b1", "late_c", [P, 3 * P + N], U32)
+        nc.vector.quantize_mx(late_c[:, :P].bitcast(FP8X4), w2_s[:, P : 2 * P], w2_b[:, 512:1024])
+        nc.vector.quantize_mx(late_c[:, P : 3 * P].bitcast(FP8X4), w2_s[:, 2 * P :], w2_b[:, 1024:])
+        a_banks = [banks[6], banks[7], banks[0], banks[1]]
         hwin = [sb("hwin%d" % t, [P, S], F32) for t in range(PACK)]
         for t in range(PACK):
             cols = slice(t * P, (t + 1) * P)
-            if t == 0:
-                codes = w2_c0[:]
-            else:
-                codes = late_c[:, (t - 1) * P : t * P]
-                nc.vector.quantize_mx(codes.bitcast(FP8X4), w2_s[:, cols], w2_b[:, t * 512 : (t + 1) * 512])
+            codes = w2_c0[:] if t == 0 else late_c[:, (t - 1) * P : t * P]
             for h in range(2):
                 hc = slice(h * HALF, (h + 1) * HALF)
-                bank = banks[1] if (t, h) == (0, 0) else a_banks[t]
+                bank = banks[2] if (t, h) == (0, 0) else a_banks[t]
                 nc.tensor.matmul_mx(bank[:, hc], lhsT=codes.bitcast(FP8X4), lhsT_scale=w2_s[:, cols],
-                                    rhs=z_c[:, hc].bitcast(FP8X4), rhs_scale=z_s[:, hc], start=True, stop=True)
+                                    rhs=z_c[h][:].bitcast(FP8X4), rhs_scale=z_s[:, hc], start=True, stop=True)
                 if t == 0:
                     nc.scalar.activation(hwin[t][:, hc], bank[:, hc], ACT.Tanh)
             if t > 0:
@@ -183,12 +183,15 @@ def tile_picked_allpass2_none_p_kernel(
             for t in range(PACK):
                 nc.vector.tensor_tensor(z2_f[:, t, :], hwin[t][:].indirect(half_list(mv_sb, h)), gains[h][:, t, :], ALU.mult)
             z2_b = shared("z2_b", "z2_b%d" % h, [P, PACK * HALF], BF16)
-            (nc.scalar.copy if h == 0 else nc.vector.tensor_copy)(woven(z2_b[:]), weave(z2_f[:]))
+            split = 0 if h == 0 else 192
+            if split:
+                nc.vector.tensor_copy(woven(z2_b[:, : PACK * split]), weave(z2_f[:, :, :split]))
+            nc.scalar.copy(woven(z2_b[:, PACK * split :]), weave(z2_f[:, :, split:]))
             nc.vector.quantize_mx(z2_c[:, hc].bitcast(FP8X4), z2_s[:, hc], z2_b[:])
         for h in range(2):
             hc = slice(h * HALF, (h + 1) * HALF)
             for a in range(2):
-                bank = banks[1 + 2 * h + a]
+                bank = banks[2 + 2 * h + a]
                 for e in range(2):
                     m = 2 * a + e
                     cols = slice(m * P, (m + 1) * P)

from contextlib import ExitStack

import concourse.mybir as mybir

F32 = mybir.dt.float32
BF16 = mybir.dt.bfloat16
I32 = mybir.dt.int32
U32 = mybir.dt.uint32
U16 = mybir.dt.uint16
U8 = mybir.dt.uint8
FP8X4 = mybir.dt.float8_e4m3fn_x4
ALU = mybir.AluOpType
ACT = mybir.ActivationFunctionType

P = 128
PACK = 4
K, T, S, N, H = 512, 2048, 512, 512, 512
FLOPS = 2 * S * (K * H + H * H + H * N)


def tile_picked_allpass2_none_p_kernel(
    tc, x_words, x_scales, w1, gn, w2, res, w3, offs, d1, d2, mv, out
):
    nc = tc.nc
    with ExitStack() as ctx:
        keep = ctx.enter_context(tc.tile_pool(name="keep", bufs=1))
        psum = ctx.enter_context(tc.psum_pool(name="psum", bufs=1))

        def sb(name, shape, dtype):
            return keep.tile(shape, dtype, name=name, align_bytes=64)

        offs_sb = sb("offs_sb", [P, S // 16], U16)
        d1_sb = sb("d1_sb", [P, S // 16], U16)
        d2_sb = sb("d2_sb", [P, S // 16], U16)
        mv_sb = sb("mv_sb", [P, S // 16], U16)
        xw = sb("xw", [P, T], I32)
        xs = sb("xs", [P, T], U8)
        xw_g = keep.tile([P, S], U32, name="xw_g", tag="xw_g", align_bytes=64)
        xs_g = keep.tile([P, S], U8, name="xs_g", tag="gains0", align_bytes=64)
        gn_sb = sb("gn_sb", [P, PACK], F32)
        gn8 = sb("gn8", [P, PACK], F32)
        gn4 = sb("gn4", [P, PACK], F32)
        w1_raw = [keep.tile([P, PACK, H // 2], F32, name="w1_raw%d" % a, tag="w_raw%d" % a, align_bytes=64) for a in range(2)]
        win = [[sb("win%d_%d" % (a, t), [P, 2 * S], F32) for t in range(PACK)] for a in range(2)]
        HALF = S // 2

        def shared(tag, name, shape, dtype):
            return keep.tile(shape, dtype, name=name, tag=tag, align_bytes=64)

        nc.vector.memset(xs[:].bitcast(I32), 0)
        xs_rows = sb("xs_rows", [P, T // 4], I32)
        for q in range(4):
            (nc.sync, nc.scalar)[q % 2].dma_start(xs_rows[32 * q : 32 * q + 4, :], x_scales[0, 4 * q : 4 * q + 4, :].bitcast(I32))
        nc.sync.dma_start(xw[:], x_words[0].rearrange("p n r -> p (n r)").bitcast(I32))
        nc.sync.dma_start(offs_sb[:], offs)
        for a in range(2):
            nc.sync.dma_start(w1_raw[a][:], w1.rearrange("(p j) c -> p j c", j=PACK)[:, :, a * (H // 2) : (a + 1) * (H // 2)])
        nc.sync.dma_start(gn_sb[:], gn.rearrange("(p t) o -> p (t o)", t=PACK))
        nc.sync.dma_start(d1_sb[:], d1)
        nc.sync.dma_start(d2_sb[:], d2)
        nc.sync.dma_start(mv_sb[:], mv)
        for t in range(PACK):
            nc.vector.memset(win[0][t][:, S:], 0.0)

        for q in range(4):
            nc.vector.tensor_copy(xs[32 * q : 32 * q + 4, :].bitcast(I32), xs_rows[32 * q : 32 * q + 4, :])
        nc.vector.tensor_copy(xs_g[:], xs[:].indirect(offs_sb[:]))
        nc.vector.tensor_copy(xw_g[:], xw[:].bitcast(U32).indirect(offs_sb[:]))

        def dealt_copy(copy, dst, raw, m0, m1, r0):
            copy(
                dst[:].rearrange("p (t m j) -> p m j t", t=PACK, j=PACK)[:, m0:m1],
                raw[:].rearrange("p j (m t) -> p m j t", t=PACK)[:, m0 - r0 : m1 - r0],
            )

        w1_b = shared("w1_b", "w1_b", [P, PACK * H], BF16)
        w1_c = sb("w1_c", [P, H], U32)
        w1_s = shared("gains1", "w1_s", [P, H], U8)
        dealt_copy(nc.scalar.copy, w1_b, w1_raw[0], 0, 64, 0)
        dealt_copy(nc.vector.tensor_copy, w1_b, w1_raw[1], 64, 108, 64)
        dealt_copy(nc.scalar.copy, w1_b, w1_raw[1], 108, 128, 64)
        nc.vector.tensor_scalar(gn8[:], gn_sb[:], 0.125, None, ALU.mult)
        nc.vector.tensor_scalar(gn4[:], gn_sb[:], 0.25, None, ALU.mult)

        banks = [psum.tile([P, S], F32, name="bank%d" % b) for b in range(8)]
        for t in range(PACK):
            cols = slice(t * P, (t + 1) * P)
            if t < 3:
                wide = slice(t * P, (t + 1) * P if t < 2 else H)
                nc.vector.quantize_mx(w1_c[:, wide].bitcast(FP8X4), w1_s[:, wide], w1_b[:, PACK * wide.start : PACK * wide.stop])
            pieces = ((0, HALF), (HALF, S)) if t == 0 else ((0, S),)
            for b, (c0, c1) in enumerate(pieces):
                bank = banks[b] if t == 0 else banks[t + 2]
                nc.tensor.matmul_mx(bank[:, : c1 - c0], lhsT=w1_c[:, cols].bitcast(FP8X4), lhsT_scale=w1_s[:, cols],
                                    rhs=xw_g[:, c0:c1].bitcast(FP8X4), rhs_scale=xs_g[:, c0:c1], start=True, stop=True)
                for dst, gain in ((win[0][t][:, c0:c1], gn8), (win[1][t][:, S + c0 : S + c1], gn4)):
                    if (t, b) == (0, 0):
                        nc.vector.tensor_scalar(dst, bank[:, : c1 - c0], gain[:, t : t + 1], None, ALU.mult)
                    else:
                        nc.scalar.activation(dst, bank[:, : c1 - c0], ACT.Copy, scale=gain[:, t : t + 1])

        w2_raw = shared("w_raw1", "w2_raw", [P, PACK, H], F32)
        w3_raw = shared("w1_b", "w3_raw", [P, PACK, N], F32)
        res_sb = shared("xw_g", "res_sb", [P, PACK, S], F32)
        nc.sync.dma_start(w2_raw[:], w2.rearrange("(p j) c -> p j c", j=PACK))
        nc.sync.dma_start(w3_raw[:], w3.rearrange("(p j) c -> p j c", j=PACK))
        nc.sync.dma_start(res_sb[:], res.rearrange("(m p) j -> p m j", p=P))

        w2_b = sb("w2_b", [P, PACK * H], BF16)
        w2_c0 = sb("w2_c0", [P, P], U32)
        w2_s = sb("w2_s", [P, H], U8)
        w3_b = sb("w3_b", [P, PACK * N], BF16)
        w3_s = sb("w3_s", [P, N], U8)
        u = [sb("u%d" % t, [P, S], F32) for t in range(PACK)]
        u_side = [shared("u_side%d" % h, "u_side%d" % h, [P, PACK, HALF], F32) for h in range(2)]

        def weave(t4):
            return t4.rearrange("p t (c i) -> p c t i", i=4)

        def woven(flat):
            return flat.rearrange("p (c i t) -> p c t i", i=4, t=PACK)

        def half_list(lst, h):
            return lst[:, h * (HALF // 16) : (h + 1) * (HALF // 16)]

        for t in range(PACK):
            nc.vector.tensor_tensor(win[1][t][:, :S], win[0][t][:].indirect(d1_sb[:]), win[1][t][:, S:], ALU.subtract)
            nc.scalar.mul(win[0][t][:, S:], win[1][t][:, :S], 0.5)
        for t in range(PACK):
            nc.vector.tensor_tensor(win[0][t][:, :S], win[1][t][:].indirect(d1_sb[:]), win[0][t][:, S:], ALU.add)
            nc.scalar.mul(win[1][t][:, S:], win[0][t][:, :S], 4.0)
            dealt_copy(nc.scalar.copy, w2_b, w2_raw, 32 * t, 32 * t + 32, 0)
        for t in range(PACK):
            nc.vector.tensor_tensor(u[t][:], win[0][t][:].indirect(d2_sb[:]), win[1][t][:, S:], ALU.subtract)
            for h in range(2):
                nc.scalar.mul(u_side[h][:, t, :], u[t][:, h * HALF : (h + 1) * HALF], 0.25)
            nc.scalar.copy(woven(w3_b[:, t * 512 : (t + 1) * 512]), weave(w3_raw[:, :, t * P : (t + 1) * P]))
        nc.vector.quantize_mx(w2_c0[:].bitcast(FP8X4), w2_s[:, :P], w2_b[:, :512])

        gains = [shared("gains%d" % h, "gains%d" % h, [P, PACK, HALF], F32) for h in range(2)]
        for h in range(2):
            for a in range(2):
                nc.scalar.copy(gains[h][:, 2 * a : 2 * a + 2], gn_sb[:, 2 * a : 2 * a + 2].unsqueeze(2).to_broadcast([P, 2, HALF]))

        z_c = []
        z_s = sb("z_s", [P, S], U8)
        for h in range(2):
            hc = slice(h * HALF, (h + 1) * HALF)
            z_f = sb("z_f", [P, PACK, HALF], F32) if h == 0 else shared("u_side0", "z_f1", [P, PACK, HALF], F32)
            for t in range(PACK):
                nc.vector.tensor_tensor(z_f[:, t, :], u[t][:].indirect(half_list(d2_sb, h)), u_side[h][:, t, :], ALU.add)
            z_b = shared("z_b%d" % h, "z_b%d" % h, [P, PACK * HALF], BF16)
            (nc.scalar.copy if h == 0 else nc.vector.tensor_copy)(woven(z_b[:]), weave(z_f[:]))
            z_c.append(sb("z_c0", [P, HALF], U32) if h == 0 else shared("z_b0", "z_c1", [P, HALF], U32))
            nc.vector.quantize_mx(z_c[h][:].bitcast(FP8X4), z_s[:, hc], z_b[:])

        late_c = shared("z_b1", "late_c", [P, 3 * P + N], U32)
        nc.vector.quantize_mx(late_c[:, :P].bitcast(FP8X4), w2_s[:, P : 2 * P], w2_b[:, 512:1024])
        nc.vector.quantize_mx(late_c[:, P : 3 * P].bitcast(FP8X4), w2_s[:, 2 * P :], w2_b[:, 1024:])
        a_banks = [banks[6], banks[7], banks[0], banks[1]]
        hwin = [sb("hwin%d" % t, [P, S], F32) for t in range(PACK)]
        for t in range(PACK):
            cols = slice(t * P, (t + 1) * P)
            codes = w2_c0[:] if t == 0 else late_c[:, (t - 1) * P : t * P]
            for h in range(2):
                hc = slice(h * HALF, (h + 1) * HALF)
                bank = banks[2] if (t, h) == (0, 0) else a_banks[t]
                nc.tensor.matmul_mx(bank[:, hc], lhsT=codes.bitcast(FP8X4), lhsT_scale=w2_s[:, cols],
                                    rhs=z_c[h][:].bitcast(FP8X4), rhs_scale=z_s[:, hc], start=True, stop=True)
                if t == 0:
                    nc.scalar.activation(hwin[t][:, hc], bank[:, hc], ACT.Tanh)
            if t > 0:
                nc.scalar.activation(hwin[t][:], a_banks[t][:], ACT.Tanh)
        w3_c = late_c[:, 3 * P :]
        nc.vector.quantize_mx(w3_c.bitcast(FP8X4), w3_s[:], w3_b[:])

        z2_c = sb("z2_c", [P, S], U32)
        z2_s = sb("z2_s", [P, S], U8)
        out_v = out.rearrange("(m p) j -> p m j", p=P)
        for h in range(2):
            hc = slice(h * HALF, (h + 1) * HALF)
            z2_f = sb("z2_f", [P, PACK, HALF], F32) if h == 0 else shared("gains0", "z2_f1", [P, PACK, HALF], F32)
            for t in range(PACK):
                nc.vector.tensor_tensor(z2_f[:, t, :], hwin[t][:].indirect(half_list(mv_sb, h)), gains[h][:, t, :], ALU.mult)
            z2_b = shared("z2_b", "z2_b%d" % h, [P, PACK * HALF], BF16)
            split = 0 if h == 0 else 192
            if split:
                nc.vector.tensor_copy(woven(z2_b[:, : PACK * split]), weave(z2_f[:, :, :split]))
            nc.scalar.copy(woven(z2_b[:, PACK * split :]), weave(z2_f[:, :, split:]))
            nc.vector.quantize_mx(z2_c[:, hc].bitcast(FP8X4), z2_s[:, hc], z2_b[:])
        for h in range(2):
            hc = slice(h * HALF, (h + 1) * HALF)
            for a in range(2):
                bank = banks[2 + 2 * h + a]
                for e in range(2):
                    m = 2 * a + e
                    cols = slice(m * P, (m + 1) * P)
                    nc.tensor.matmul_mx(bank[:, e * HALF : (e + 1) * HALF], lhsT=w3_c[:, cols].bitcast(FP8X4), lhsT_scale=w3_s[:, cols],
                                        rhs=z2_c[:, hc].bitcast(FP8X4), rhs_scale=z2_s[:, hc], start=True, stop=True)
                for e0, e1 in ((0, 1), (1, 2)) if (h, a) == (1, 1) else ((0, 2),):
                    o_sb = sb("o_sb%d_%d_%d" % (h, a, e0), [P, e1 - e0, HALF], F32)
                    rows = slice(2 * a + e0, 2 * a + e1)
                    nc.vector.tensor_tensor(o_sb[:], bank[:].rearrange("p (e j) -> p e j", e=2)[:, e0:e1], res_sb[:, rows, hc], ALU.add)
                    nc.sync.dma_start(out_v[:, rows, hc], o_sb[:])
